import numpy as np
import ml_dtypes


def mxq(x, axis, fmt="e4m3"):
    dtype, down = {"e4m3": (ml_dtypes.float8_e4m3fn, 7), "e5m2": (ml_dtypes.float8_e5m2, 14)}[fmt]
    v = np.moveaxis(np.asarray(x, np.float32).astype(ml_dtypes.bfloat16).astype(np.float64), axis, -1)
    blocks = v.reshape(v.shape[:-1] + (-1, 32))
    amax = np.abs(blocks).max(-1, keepdims=True)
    byte = np.maximum(np.where(amax > 0, np.frexp(amax)[1] - 1 + 127, 0) - down, 1)
    scale = np.exp2(byte - 127.0)
    codes = (blocks / scale).astype(np.float32).astype(dtype).astype(np.float64)
    return np.moveaxis((codes * scale).reshape(v.shape), -1, axis)


WIDE = False


def mx_kscale(k):
    if not WIDE:
        return np.ones(k)
    levels = np.array([30, -30])
    if k % 512:
        return np.exp2(np.random.permutation(np.resize(levels, k // 32))).repeat(32)
    a = np.empty((k // 512, 16))
    for p in range(k // 512):
        a[p, :8] = np.random.permutation(np.resize(levels, 8))
        for g in range(8):
            far = levels[np.abs(levels - a[p, g]) >= 10]
            a[p, g + 8] = far[np.random.randint(len(far))]
    return np.exp2(a.ravel()).repeat(32)


def f64(x):
    return np.asarray(x).astype(np.float64)


def striped(idx):
    return np.tile(np.asarray(idx).reshape(-1, 16).T, (8, 1)).astype(np.uint16)


def unstriped(offs):
    return offs[:16].T.reshape(-1).astype(np.int64)


E2M1 = np.array([0.0, 0.5, 1.0, 1.5, 2.0, 3.0, 4.0, 6.0, -0.0, -0.5, -1.0, -1.5, -2.0, -3.0, -4.0, -6.0])


def pack_weight(w, fmt):
    k, n = w.shape
    w = f64(np.asarray(w, np.float32).astype(ml_dtypes.bfloat16)).reshape(k // 32, 32, n)
    amax = np.abs(w).max(1)
    if fmt in ("e4m3", "e5m2"):
        byte = np.frexp(amax)[1] - 1 + 127 - (7 if fmt == "e4m3" else 14)
    else:
        mant, ex = np.frexp(amax / 6.0)
        byte = np.where(mant > 0.5, ex, ex - 1) + 127
    byte = np.clip(np.where(amax > 0, byte, 1), 1, 254)
    scaled = (w * np.exp2(127.0 - byte)[:, None, :]).reshape(k, n).astype(np.float32)
    by_word = np.ascontiguousarray(scaled.reshape(k // 512, 128, 4, n).transpose(0, 1, 3, 2))
    if fmt in ("e4m3", "e5m2"):
        words = by_word.astype(ml_dtypes.float8_e4m3fn if fmt == "e4m3" else ml_dtypes.float8_e5m2).view(np.uint8)
    else:
        c = by_word.astype(ml_dtypes.float4_e2m1fn).view(np.uint8) & 0xF
        words = (c[..., 0::2] | (c[..., 1::2] << 4)).reshape(k // 512, 128, 2 * n)
    return np.ascontiguousarray(words), np.ascontiguousarray(byte.astype(np.uint8).reshape(k // 512, 16, n))


def unpack_weight(words, scales, fmt):
    g, _, n = scales.shape
    words = np.ascontiguousarray(words).reshape(g, 128, n, -1)
    if fmt in ("e4m3", "e5m2"):
        vals = words.view(ml_dtypes.float8_e4m3fn if fmt == "e4m3" else ml_dtypes.float8_e5m2).astype(np.float64)
    else:
        nib = np.empty((g, 128, n, 4), np.uint8)
        nib[..., 0::2] = words & 0xF
        nib[..., 1::2] = words >> 4
        vals = E2M1[nib]
    vals = vals * np.repeat(np.exp2(scales.astype(np.float64) - 127.0), 8, axis=1)[..., None]
    return vals.transpose(0, 1, 3, 2).reshape(g * 512, n)


K, T, J, R, C, O, N = 512, 1024, 256, 512, 512, 128, 256


def setup_inputs():
    n = np.random.standard_normal
    idx = np.random.permutation(T)[:J]
    idx2 = np.random.permutation(C)[:J]
    idx3 = np.random.permutation(C)[:O]
    idx4 = np.random.permutation(J)[:O]
    idx5 = np.random.permutation(T)[:O]
    fk = mx_kscale(K)
    fr = mx_kscale(R)
    xtp = pack_weight(n((K, T)) / fk[:, None], "e5m2")
    wp = pack_weight(n((K, R)) * 1 / np.sqrt(K) * fk[:, None] * fr, "e2m1")
    w2p = pack_weight(n((K, R)) * 1 / np.sqrt(K) * fk[:, None] * fr, "e4m3")
    wbp = pack_weight(n((R, N)) * 1 / np.sqrt(R) / fr[:, None], "e2m1")
    wsp = pack_weight(n((K, N)) * 1 / np.sqrt(K) * fk[:, None], "e2m1")
    return {
        "xt_words": xtp[0],
        "xt_scales": xtp[1],
        "w_words": wp[0],
        "w_scales": wp[1],
        "w2_words": w2p[0],
        "w2_scales": w2p[1],
        "sa": (np.random.uniform(0.5, 1.6, (R, 1))).astype(np.float32),
        "wb_words": wbp[0],
        "wb_scales": wbp[1],
        "ws_words": wsp[0],
        "ws_scales": wsp[1],
        "offs": striped(idx),
        "offs2": striped(idx2),
        "offs3": striped(idx3),
        "offs4": striped(idx4),
        "offs5": striped(idx5),
    }


def reference(xt_words, xt_scales, w_words, w_scales, w2_words, w2_scales, sa, wb_words, wb_scales, ws_words, ws_scales, offs, offs2, offs3, offs4, offs5):
    idx = unstriped(offs)
    idx2 = unstriped(offs2)
    idx3 = unstriped(offs3)
    idx4 = unstriped(offs4)
    idx5 = unstriped(offs5)
    xtu = unpack_weight(xt_words, xt_scales, "e5m2")
    wu = unpack_weight(w_words, w_scales, "e2m1")
    w2u = unpack_weight(w2_words, w2_scales, "e4m3")
    wbu = unpack_weight(wb_words, wb_scales, "e2m1")
    wsu = unpack_weight(ws_words, ws_scales, "e2m1")
    xtidxg = xtu[:, idx]
    a = wu.T @ xtidxg
    b = w2u.T @ xtidxg
    pw = np.zeros((R, C))
    pw[:, idx2] = a
    hid = np.maximum(pw[:, idx3] * f64(sa), b[:, idx4])
    hidq = mxq(hid, 0, "e4m3")
    xtidx5g = xtu[:, idx5]
    y = wbu.T @ hidq + wsu.T @ xtidx5g
    return y

@@ -1,0 +1,217 @@
+from contextlib import ExitStack
+
+import concourse.mybir as mybir
+
+K, T, J, R, C, O, N = 512, 1024, 256, 512, 512, 128, 256
+FLOPS = 2 * K * J * R * 2 + 2 * N * O * (R + K)
+
+F32 = mybir.dt.float32
+BF16 = mybir.dt.bfloat16
+I32 = mybir.dt.int32
+U32 = mybir.dt.uint32
+U16 = mybir.dt.uint16
+U8 = mybir.dt.uint8
+E4M3 = mybir.dt.float8_e4m3fn_x4
+E5M2 = mybir.dt.float8_e5m2_x4
+E2M1 = mybir.dt.float4_e2m1fn_x4
+COPY = mybir.ActivationFunctionType.Copy
+MAX = mybir.AluOpType.max
+
+P = 128
+PACK = 4
+QUADS = 4
+
+
+def load_scale_rows(queue, plane, scales):
+    for q in range(QUADS):
+        queue.dma_start(
+            out=plane[32 * q : 32 * q + 4, :].bitcast(I32),
+            in_=scales[0, 4 * q : 4 * q + 4, :].bitcast(I32),
+        )
+
+
+def tile_list_boardweighed_twow_further_plain_kernel(
+    tc, xt_words, xt_scales, w_words, w_scales, w2_words, w2_scales, sa, wb_words, wb_scales,
+    ws_words, ws_scales, offs, offs2, offs3, offs4, offs5, out,
+):
+    nc = tc.nc
+    with ExitStack() as ctx:
+        lists = ctx.enter_context(tc.tile_pool(name="lists", bufs=1))
+        sb = ctx.enter_context(tc.tile_pool(name="sb", bufs=1))
+        ps = ctx.enter_context(tc.psum_pool(name="ps", bufs=1))
+
+        l_tok = lists.tile([P, J // 16], U16, name="l_tok")
+        l_put = lists.tile([P, J // 16], U16, name="l_put")
+        l_board = lists.tile([P, O // 16], U16, name="l_board")
+        l_slot = lists.tile([P, O // 16], U16, name="l_slot")
+        l_short = lists.tile([P, O // 16], U16, name="l_short")
+
+        xw = sb.tile([P, T], I32, name="xw", align_bytes=64)
+        xs = sb.tile([P, T], U8, name="xs", align_bytes=64)
+        ww = sb.tile([P, 2 * R], U8, name="ww", align_bytes=64)
+        wsc = sb.tile([P, R], U8, name="wsc", align_bytes=64)
+        wst = sb.tile([4, QUADS, R], U8, name="wst", align_bytes=64)
+        w2w = sb.tile([P, R], I32, name="w2w", align_bytes=64)
+        w2s = sb.tile([P, R], U8, name="w2s", align_bytes=64)
+        wbw = sb.tile([P, 2 * N], U8, name="wbw", align_bytes=64)
+        wbs = sb.tile([P, N], U8, name="wbs", align_bytes=64)
+        wsw = sb.tile([P, 2 * N], U8, name="wsw", align_bytes=64)
+        wss = sb.tile([P, N], U8, name="wss", align_bytes=64)
+        sa_sb = sb.tile([P, PACK], F32, name="sa_sb", align_bytes=64)
+        boards = [sb.tile([P, C], F32, name="board%d" % t, align_bytes=64) for t in range(PACK)]
+
+        nc.gpsimd.memset(wsc[:].bitcast(I32), 0)
+        nc.gpsimd.memset(w2s[:].bitcast(I32), 0)
+        nc.gpsimd.memset(wbs[:].bitcast(I32), 0)
+        nc.gpsimd.memset(wss[:].bitcast(I32), 0)
+        for t in range(PACK):
+            nc.vector.memset(boards[t][:], 0.0)
+
+        nc.sync.dma_start(
+            out=wst[:].bitcast(I32),
+            in_=w_scales[0].bitcast(I32).rearrange("(q r) c -> r q c", r=4),
+        )
+        for q in range(QUADS):
+            queue = nc.sync if q == 0 else nc.scalar
+            queue.dma_start(
+                out=xs[32 * q : 32 * q + 32, :].bitcast(I32),
+                in_=xt_scales[0, 4 * q : 4 * q + 4, :].bitcast(I32).partition_broadcast(8),
+            )
+        nc.sync.dma_start(l_tok[:], offs)
+        nc.scalar.dma_start(out=xw[:], in_=xt_words[0].rearrange("p n t -> p (n t)").bitcast(I32))
+        nc.sync.dma_start(out=ww[:].bitcast(I32), in_=w_words[0].bitcast(I32))
+        nc.sync.dma_start(l_short[:], offs5)
+        nc.sync.dma_start(l_put[:], offs2)
+        nc.sync.dma_start(out=w2w[:], in_=w2_words[0].rearrange("p n t -> p (n t)").bitcast(I32))
+        load_scale_rows(nc.sync, w2s, w2_scales)
+        nc.sync.dma_start(l_board[:], offs3)
+        nc.sync.dma_start(out=sa_sb[:], in_=sa.rearrange("(p t) o -> p (t o)", t=PACK))
+        nc.sync.dma_start(l_slot[:], offs4)
+        nc.sync.dma_start(out=wsw[:].bitcast(I32), in_=ws_words[0].bitcast(I32))
+        load_scale_rows(nc.sync, wss, ws_scales)
+        nc.sync.dma_start(out=wbw[:].bitcast(I32), in_=wb_words[0].bitcast(I32))
+        load_scale_rows(nc.sync, wbs, wb_scales)
+
+        for q in range(QUADS):
+            nc.vector.tensor_copy(
+                out=wsc[32 * q : 32 * q + 4, :].bitcast(I32), in_=wst[:, q, :].bitcast(I32)
+            )
+        wwp = sb.tile([P, 2 * R], U8, name="wwp", align_bytes=64)
+        wsp = sb.tile([P, R], U8, name="wsp", align_bytes=64)
+        nc.scalar.copy(
+            out=wwp[:].bitcast(U16).rearrange("p (t m) -> p t m", t=PACK),
+            in_=ww[:].bitcast(U16).rearrange("p (m t) -> p t m", t=PACK),
+        )
+
+        xgs = sb.tile([P, J], U8, name="xgs", align_bytes=64)
+        xgw = sb.tile([P, J], U32, name="xgw", align_bytes=64)
+        nc.vector.tensor_copy(xgs[:], xs[:].indirect(l_tok[:]))
+        nc.vector.tensor_copy(
+            out=wsp[:].rearrange("p (t m) -> p t m", t=PACK),
+            in_=wsc[:].rearrange("p (m t) -> p t m", t=PACK),
+        )
+        nc.vector.tensor_copy(xgw[:], xw[:].bitcast(U32).indirect(l_tok[:]))
+
+        a_ps = [ps.tile([P, J], F32, name="a_ps%d" % t) for t in range(PACK)]
+        for t in range(PACK):
+            nc.tensor.matmul_mx(
+                out=a_ps[t][:],
+                lhsT=wwp[:, 2 * P * t : 2 * P * (t + 1)].bitcast(E2M1),
+                lhsT_scale=wsp[:, P * t : P * (t + 1)],
+                rhs=xgw[:].bitcast(E5M2),
+                rhs_scale=xgs[:],
+                start=True,
+                stop=True,
+            )
+
+        x5s = sb.tile([P, O], U8, name="x5s", align_bytes=64)
+        x5w = sb.tile([P, O], U32, name="x5w", align_bytes=64)
+        nc.vector.tensor_copy(x5s[:], xs[:].indirect(l_short[:]))
+        nc.vector.tensor_copy(x5w[:], xw[:].bitcast(U32).indirect(l_short[:]))
+
+        w2wp = sb.tile([P, R], I32, name="w2wp", align_bytes=64)
+        w2sp = sb.tile([P, R], U8, name="w2sp", align_bytes=64)
+        nc.gpsimd.tensor_copy(
+            out=w2wp[:].rearrange("p (t m) -> p t m", t=PACK),
+            in_=w2w[:].rearrange("p (m t) -> p t m", t=PACK),
+        )
+        nc.gpsimd.tensor_copy(
+            out=w2sp[:].rearrange("p (t m) -> p t m", t=PACK),
+            in_=w2s[:].rearrange("p (m t) -> p t m", t=PACK),
+        )
+        b_ps = [ps.tile([P, 2, J], F32, name="b_ps%d" % h) for h in range(2)]
+        for t in range(PACK):
+            nc.tensor.matmul_mx(
+                out=b_ps[t // 2][:, t % 2, :],
+                lhsT=w2wp[:, P * t : P * (t + 1)].bitcast(E4M3),
+                lhsT_scale=w2sp[:, P * t : P * (t + 1)],
+                rhs=xgw[:].bitcast(E5M2),
+                rhs_scale=xgs[:],
+                start=True,
+                stop=True,
+            )
+        y_ps = [ps.tile([P, O], F32, name="y_ps%d" % h) for h in range(2)]
+        for h in range(2):
+            nc.tensor.matmul_mx(
+                out=y_ps[h][:],
+                lhsT=wsw[:, 2 * P * h : 2 * P * (h + 1)].bitcast(E2M1),
+                lhsT_scale=wss[:, P * h : P * (h + 1)],
+                rhs=x5w[:].bitcast(E5M2),
+                rhs_scale=x5s[:],
+                start=True,
+                stop=False,
+            )
+
+        a_sb = [sb.tile([P, J], F32, name="a_sb%d" % t, align_bytes=64) for t in range(PACK)]
+        for t in range(PACK):
+            if t % 2 == 1:
+                nc.vector.tensor_copy(a_sb[t][:], a_ps[t][:])
+            else:
+                nc.scalar.activation(a_sb[t][:], a_ps[t][:], COPY)
+        for t in range(PACK):
+            if t % 2 == 1:
+                nc.vector.tensor_copy(boards[t][:].indirect(l_put[:]), a_sb[t][:])
+            else:
+                nc.scalar.activation(boards[t][:].indirect(l_put[:]), a_sb[t][:], COPY)
+
+        pg = sb.tile([P, PACK, O], F32, name="pg", align_bytes=64)
+        for t in range(PACK):
+            nc.scalar.activation(
+                pg[:, t, :], boards[t][:].indirect(l_board[:]), COPY, scale=sa_sb[:, t : t + 1]
+            )
+        b_sb = [sb.tile([P, 2, J], F32, name="b_sb%d" % h, align_bytes=64) for h in range(2)]
+        bg = sb.tile([P, PACK, O], F32, name="bg", align_bytes=64)
+        nc.vector.tensor_copy(b_sb[0][:], b_ps[0][:])
+        nc.vector.tensor_copy(b_sb[1][:], b_ps[1][:])
+        for t in range(PACK):
+            if t < 2:
+                nc.scalar.activation(bg[:, t, :], b_sb[t // 2][:, t % 2, :].indirect(l_slot[:]), COPY)
+            else:
+                nc.vector.tensor_copy(bg[:, t, :], b_sb[t // 2][:, t % 2, :].indirect(l_slot[:]))
+
+        hid = sb.tile([P, O, PACK], BF16, name="hid", align_bytes=64)
+        nc.vector.tensor_tensor(
+            hid[:].rearrange("p (c i) t -> p c t i", i=4),
+            pg[:].rearrange("p t (c i) -> p c t i", i=4),
+            bg[:].rearrange("p t (c i) -> p c t i", i=4),
+            MAX,
+        )
+        hq = sb.tile([P, O], U32, name="hq", align_bytes=64)
+        hs = sb.tile([P, O], U8, name="hs", align_bytes=64)
+        nc.vector.quantize_mx(out=hq[:].bitcast(E4M3), scales=hs[:], in_=hid[:].rearrange("p o t -> p (o t)"))
+
+        y_sb = [sb.tile([P, O], F32, name="y_sb%d" % h, align_bytes=64) for h in range(2)]
+        for h in range(2):
+            nc.tensor.matmul_mx(
+                out=y_ps[h][:],
+                lhsT=wbw[:, 2 * P * h : 2 * P * (h + 1)].bitcast(E2M1),
+                lhsT_scale=wbs[:, P * h : P * (h + 1)],
+                rhs=hq[:].bitcast(E4M3),
+                rhs_scale=hs[:],
+                start=False,
+                stop=True,
+            )
+        nc.vector.tensor_copy(y_sb[0][:], y_ps[0][:])
+        nc.sync.dma_start(out=out[0:P, :], in_=y_sb[0][:])
+        nc.scalar.activation(y_sb[1][:], y_ps[1][:], COPY)
+        nc.scalar.dma_start(out=out[P : 2 * P, :], in_=y_sb[1][:])

@@ -46,10 +46,10 @@ def tile_list_boardweighed_twow_further_plain_kernel(
         l_slot = lists.tile([P, O // 16], U16, name="l_slot")
         l_short = lists.tile([P, O // 16], U16, name="l_short")
 
-        xw = sb.tile([P, T], I32, name="xw", align_bytes=64)
-        xs = sb.tile([P, T], U8, name="xs", align_bytes=64)
-        ww = sb.tile([P, 2 * R], U8, name="ww", align_bytes=64)
-        wsc = sb.tile([P, R], U8, name="wsc", align_bytes=64)
+        xw = sb.tile([P, T], I32, name="xw", tag="a3", align_bytes=64)
+        xs = sb.tile([P, T], U8, name="xs", tag="a1", align_bytes=64)
+        ww = sb.tile([P, 2 * R], U8, name="ww", tag="ww", align_bytes=64)
+        wsc = sb.tile([P, R], U8, name="wsc", tag="dealt_scales", align_bytes=64)
         wst = sb.tile([4, QUADS, R], U8, name="wst", align_bytes=64)
         w2w = sb.tile([P, R], I32, name="w2w", align_bytes=64)
         w2s = sb.tile([P, R], U8, name="w2s", align_bytes=64)
@@ -71,19 +71,19 @@ def tile_list_boardweighed_twow_further_plain_kernel(
             out=wst[:].bitcast(I32),
             in_=w_scales[0].bitcast(I32).rearrange("(q r) c -> r q c", r=4),
         )
+        nc.sync.dma_start(l_tok[:], offs)
         for q in range(QUADS):
             queue = nc.sync if q == 0 else nc.scalar
             queue.dma_start(
                 out=xs[32 * q : 32 * q + 32, :].bitcast(I32),
                 in_=xt_scales[0, 4 * q : 4 * q + 4, :].bitcast(I32).partition_broadcast(8),
             )
-        nc.sync.dma_start(l_tok[:], offs)
-        nc.scalar.dma_start(out=xw[:], in_=xt_words[0].rearrange("p n t -> p (n t)").bitcast(I32))
-        nc.sync.dma_start(out=ww[:].bitcast(I32), in_=w_words[0].bitcast(I32))
+        nc.sync.dma_start(out=xw[:], in_=xt_words[0].rearrange("p n t -> p (n t)").bitcast(I32))
+        nc.scalar.dma_start(out=ww[:].bitcast(I32), in_=w_words[0].bitcast(I32))
         nc.sync.dma_start(l_short[:], offs5)
         nc.sync.dma_start(l_put[:], offs2)
-        nc.sync.dma_start(out=w2w[:], in_=w2_words[0].rearrange("p n t -> p (n t)").bitcast(I32))
         load_scale_rows(nc.sync, w2s, w2_scales)
+        nc.sync.dma_start(out=w2w[:], in_=w2_words[0].rearrange("p n t -> p (n t)").bitcast(I32))
         nc.sync.dma_start(l_board[:], offs3)
         nc.sync.dma_start(out=sa_sb[:], in_=sa.rearrange("(p t) o -> p (t o)", t=PACK))
         nc.sync.dma_start(l_slot[:], offs4)
@@ -98,15 +98,15 @@ def tile_list_boardweighed_twow_further_plain_kernel(
             )
         wwp = sb.tile([P, 2 * R], U8, name="wwp", align_bytes=64)
         wsp = sb.tile([P, R], U8, name="wsp", align_bytes=64)
-        nc.scalar.copy(
-            out=wwp[:].bitcast(U16).rearrange("p (t m) -> p t m", t=PACK),
-            in_=ww[:].bitcast(U16).rearrange("p (m t) -> p t m", t=PACK),
-        )
+        dealt = wwp[:].bitcast(U16).rearrange("p (t m) -> p t m", t=PACK)
+        given = ww[:].bitcast(U16).rearrange("p (m t) -> p t m", t=PACK)
+        nc.scalar.copy(out=dealt[:, 0:1, :], in_=given[:, 0:1, :])
+        nc.scalar.copy(out=dealt[:, 1:PACK, :], in_=given[:, 1:PACK, :])
 
         xgs = sb.tile([P, J], U8, name="xgs", align_bytes=64)
         xgw = sb.tile([P, J], U32, name="xgw", align_bytes=64)
         nc.vector.tensor_copy(xgs[:], xs[:].indirect(l_tok[:]))
-        nc.vector.tensor_copy(
+        nc.gpsimd.tensor_copy(
             out=wsp[:].rearrange("p (t m) -> p t m", t=PACK),
             in_=wsc[:].rearrange("p (m t) -> p t m", t=PACK),
         )
@@ -124,22 +124,22 @@ def tile_list_boardweighed_twow_further_plain_kernel(
                 stop=True,
             )
 
-        x5s = sb.tile([P, O], U8, name="x5s", align_bytes=64)
+        x5s = sb.tile([P, O], U8, name="x5s", tag="ww", align_bytes=64)
         x5w = sb.tile([P, O], U32, name="x5w", align_bytes=64)
         nc.vector.tensor_copy(x5s[:], xs[:].indirect(l_short[:]))
         nc.vector.tensor_copy(x5w[:], xw[:].bitcast(U32).indirect(l_short[:]))
 
         w2wp = sb.tile([P, R], I32, name="w2wp", align_bytes=64)
-        w2sp = sb.tile([P, R], U8, name="w2sp", align_bytes=64)
-        nc.gpsimd.tensor_copy(
-            out=w2wp[:].rearrange("p (t m) -> p t m", t=PACK),
-            in_=w2w[:].rearrange("p (m t) -> p t m", t=PACK),
-        )
+        w2sp = sb.tile([P, R], U8, name="w2sp", tag="dealt_scales", align_bytes=64)
         nc.gpsimd.tensor_copy(
             out=w2sp[:].rearrange("p (t m) -> p t m", t=PACK),
             in_=w2s[:].rearrange("p (m t) -> p t m", t=PACK),
         )
-        b_ps = [ps.tile([P, 2, J], F32, name="b_ps%d" % h) for h in range(2)]
+        nc.gpsimd.tensor_copy(
+            out=w2wp[:].rearrange("p (t m) -> p t m", t=PACK),
+            in_=w2w[:].rearrange("p (m t) -> p t m", t=PACK),
+        )
+        b_ps = [ps.tile([P, 2, J], F32, name="b_ps%d" % h, tag="bank%d" % h) for h in range(2)]
         for t in range(PACK):
             nc.tensor.matmul_mx(
                 out=b_ps[t // 2][:, t % 2, :],
@@ -150,7 +150,30 @@ def tile_list_boardweighed_twow_further_plain_kernel(
                 start=True,
                 stop=True,
             )
-        y_ps = [ps.tile([P, O], F32, name="y_ps%d" % h) for h in range(2)]
+
+        a_sb = [sb.tile([P, J], F32, name="a_sb%d" % t, tag="a%d" % t, align_bytes=64) for t in range(PACK)]
+        for t in range(PACK):
+            if t % 2 == 1:
+                nc.vector.tensor_copy(a_sb[t][:], a_ps[t][:])
+                nc.vector.tensor_copy(boards[t][:].indirect(l_put[:]), a_sb[t][:])
+            else:
+                nc.scalar.activation(a_sb[t][:], a_ps[t][:], COPY)
+                nc.scalar.activation(boards[t][:].indirect(l_put[:]), a_sb[t][:], COPY)
+
+        pg = sb.tile([P, PACK, O], F32, name="pg", align_bytes=64)
+        b_sb = [sb.tile([P, 2, J], F32, name="b_sb%d" % h, align_bytes=64) for h in range(2)]
+        bg = sb.tile([P, PACK, O], F32, name="bg", align_bytes=64)
+        for t in (0, 2, 1, 3):
+            nc.scalar.activation(
+                pg[:, t, :], boards[t][:].indirect(l_board[:]), COPY, scale=sa_sb[:, t : t + 1]
+            )
+        for h in range(2):
+            nc.vector.tensor_copy(b_sb[h][:], b_ps[h][:])
+        nc.scalar.activation(bg[:, 0, :], b_sb[0][:, 0, :].indirect(l_slot[:]), COPY)
+        for t in range(1, PACK):
+            nc.vector.tensor_copy(bg[:, t, :], b_sb[t // 2][:, t % 2, :].indirect(l_slot[:]))
+
+        y_ps = [ps.tile([P, O], F32, name="y_ps%d" % h, tag="bank%d" % h) for h in range(2)]
         for h in range(2):
             nc.tensor.matmul_mx(
                 out=y_ps[h][:],
@@ -161,33 +184,6 @@ def tile_list_boardweighed_twow_further_plain_kernel(
                 start=True,
                 stop=False,
             )
-
-        a_sb = [sb.tile([P, J], F32, name="a_sb%d" % t, align_bytes=64) for t in range(PACK)]
-        for t in range(PACK):
-            if t % 2 == 1:
-                nc.vector.tensor_copy(a_sb[t][:], a_ps[t][:])
-            else:
-                nc.scalar.activation(a_sb[t][:], a_ps[t][:], COPY)
-        for t in range(PACK):
-            if t % 2 == 1:
-                nc.vector.tensor_copy(boards[t][:].indirect(l_put[:]), a_sb[t][:])
-            else:
-                nc.scalar.activation(boards[t][:].indirect(l_put[:]), a_sb[t][:], COPY)
-
-        pg = sb.tile([P, PACK, O], F32, name="pg", align_bytes=64)
-        for t in range(PACK):
-            nc.scalar.activation(
-                pg[:, t, :], boards[t][:].indirect(l_board[:]), COPY, scale=sa_sb[:, t : t + 1]
-            )
-        b_sb = [sb.tile([P, 2, J], F32, name="b_sb%d" % h, align_bytes=64) for h in range(2)]
-        bg = sb.tile([P, PACK, O], F32, name="bg", align_bytes=64)
-        nc.vector.tensor_copy(b_sb[0][:], b_ps[0][:])
-        nc.vector.tensor_copy(b_sb[1][:], b_ps[1][:])
-        for t in range(PACK):
-            if t < 2:
-                nc.scalar.activation(bg[:, t, :], b_sb[t // 2][:, t % 2, :].indirect(l_slot[:]), COPY)
-            else:
-                nc.vector.tensor_copy(bg[:, t, :], b_sb[t // 2][:, t % 2, :].indirect(l_slot[:]))
 
         hid = sb.tile([P, O, PACK], BF16, name="hid", align_bytes=64)
         nc.vector.tensor_tensor(

@@ -30,6 +30,13 @@ def load_scale_rows(queue, plane, scales):
         )
 
 
+def deal_columns(copy, dealt, given, run, slices):
+    copy(
+        out=dealt.rearrange("p (t c i) -> p c t i", t=PACK, i=run)[:, :, slices, :],
+        in_=given.rearrange("p (c i t) -> p c t i", t=PACK, i=run)[:, :, slices, :],
+    )
+
+
 def tile_list_boardweighed_twow_further_plain_kernel(
     tc, xt_words, xt_scales, w_words, w_scales, w2_words, w2_scales, sa, wb_words, wb_scales,
     ws_words, ws_scales, offs, offs2, offs3, offs4, offs5, out,
@@ -49,7 +56,7 @@ def tile_list_boardweighed_twow_further_plain_kernel(
         xw = sb.tile([P, T], I32, name="xw", tag="a3", align_bytes=64)
         xs = sb.tile([P, T], U8, name="xs", tag="a1", align_bytes=64)
         ww = sb.tile([P, 2 * R], U8, name="ww", tag="ww", align_bytes=64)
-        wsc = sb.tile([P, R], U8, name="wsc", tag="dealt_scales", align_bytes=64)
+        wsc = sb.tile([P, R], U8, name="wsc", align_bytes=64)
         wst = sb.tile([4, QUADS, R], U8, name="wst", align_bytes=64)
         w2w = sb.tile([P, R], I32, name="w2w", align_bytes=64)
         w2s = sb.tile([P, R], U8, name="w2s", align_bytes=64)
@@ -60,6 +67,7 @@ def tile_list_boardweighed_twow_further_plain_kernel(
         sa_sb = sb.tile([P, PACK], F32, name="sa_sb", align_bytes=64)
         boards = [sb.tile([P, C], F32, name="board%d" % t, align_bytes=64) for t in range(PACK)]
 
+        nc.gpsimd.memset(xs[:].bitcast(I32), 0)
         nc.gpsimd.memset(wsc[:].bitcast(I32), 0)
         nc.gpsimd.memset(w2s[:].bitcast(I32), 0)
         nc.gpsimd.memset(wbs[:].bitcast(I32), 0)
@@ -72,14 +80,9 @@ def tile_list_boardweighed_twow_further_plain_kernel(
             in_=w_scales[0].bitcast(I32).rearrange("(q r) c -> r q c", r=4),
         )
         nc.sync.dma_start(l_tok[:], offs)
-        for q in range(QUADS):
-            queue = nc.sync if q == 0 else nc.scalar
-            queue.dma_start(
-                out=xs[32 * q : 32 * q + 32, :].bitcast(I32),
-                in_=xt_scales[0, 4 * q : 4 * q + 4, :].bitcast(I32).partition_broadcast(8),
-            )
+        load_scale_rows(nc.scalar, xs, xt_scales)
         nc.sync.dma_start(out=xw[:], in_=xt_words[0].rearrange("p n t -> p (n t)").bitcast(I32))
-        nc.scalar.dma_start(out=ww[:].bitcast(I32), in_=w_words[0].bitcast(I32))
+        nc.sync.dma_start(out=ww[:].bitcast(I32), in_=w_words[0].bitcast(I32))
         nc.sync.dma_start(l_short[:], offs5)
         nc.sync.dma_start(l_put[:], offs2)
         load_scale_rows(nc.sync, w2s, w2_scales)
@@ -98,18 +101,13 @@ def tile_list_boardweighed_twow_further_plain_kernel(
             )
         wwp = sb.tile([P, 2 * R], U8, name="wwp", align_bytes=64)
         wsp = sb.tile([P, R], U8, name="wsp", align_bytes=64)
-        dealt = wwp[:].bitcast(U16).rearrange("p (t m) -> p t m", t=PACK)
-        given = ww[:].bitcast(U16).rearrange("p (m t) -> p t m", t=PACK)
-        nc.scalar.copy(out=dealt[:, 0:1, :], in_=given[:, 0:1, :])
-        nc.scalar.copy(out=dealt[:, 1:PACK, :], in_=given[:, 1:PACK, :])
+        deal_columns(nc.scalar.copy, wwp[:].bitcast(U16), ww[:].bitcast(U16), 8, slice(0, 2))
+        deal_columns(nc.scalar.copy, wwp[:].bitcast(U16), ww[:].bitcast(U16), 8, slice(2, 4))
+        deal_columns(nc.vector.tensor_copy, wsp[:], wsc[:], 16, slice(0, 4))
 
         xgs = sb.tile([P, J], U8, name="xgs", align_bytes=64)
         xgw = sb.tile([P, J], U32, name="xgw", align_bytes=64)
         nc.vector.tensor_copy(xgs[:], xs[:].indirect(l_tok[:]))
-        nc.gpsimd.tensor_copy(
-            out=wsp[:].rearrange("p (t m) -> p t m", t=PACK),
-            in_=wsc[:].rearrange("p (m t) -> p t m", t=PACK),
-        )
         nc.vector.tensor_copy(xgw[:], xw[:].bitcast(U32).indirect(l_tok[:]))
 
         a_ps = [ps.tile([P, J], F32, name="a_ps%d" % t) for t in range(PACK)]
@@ -130,15 +128,9 @@ def tile_list_boardweighed_twow_further_plain_kernel(
         nc.vector.tensor_copy(x5w[:], xw[:].bitcast(U32).indirect(l_short[:]))
 
         w2wp = sb.tile([P, R], I32, name="w2wp", align_bytes=64)
-        w2sp = sb.tile([P, R], U8, name="w2sp", tag="dealt_scales", align_bytes=64)
-        nc.gpsimd.tensor_copy(
-            out=w2sp[:].rearrange("p (t m) -> p t m", t=PACK),
-            in_=w2s[:].rearrange("p (m t) -> p t m", t=PACK),
-        )
-        nc.gpsimd.tensor_copy(
-            out=w2wp[:].rearrange("p (t m) -> p t m", t=PACK),
-            in_=w2w[:].rearrange("p (m t) -> p t m", t=PACK),
-        )
+        w2sp = sb.tile([P, R], U8, name="w2sp", align_bytes=64)
+        deal_columns(nc.gpsimd.tensor_copy, w2sp[:], w2s[:], 16, slice(0, 4))
+        deal_columns(nc.gpsimd.tensor_copy, w2wp[:], w2w[:], 4, slice(0, 4))
         b_ps = [ps.tile([P, 2, J], F32, name="b_ps%d" % h, tag="bank%d" % h) for h in range(2)]
         for t in range(PACK):
             nc.tensor.matmul_mx(
@@ -155,9 +147,12 @@ def tile_list_boardweighed_twow_further_plain_kernel(
         for t in range(PACK):
             if t % 2 == 1:
                 nc.vector.tensor_copy(a_sb[t][:], a_ps[t][:])
-                nc.vector.tensor_copy(boards[t][:].indirect(l_put[:]), a_sb[t][:])
             else:
                 nc.scalar.activation(a_sb[t][:], a_ps[t][:], COPY)
+        for t in range(PACK):
+            if t % 2 == 1:
+                nc.vector.tensor_copy(boards[t][:].indirect(l_put[:]), a_sb[t][:])
+            else:
                 nc.scalar.activation(boards[t][:].indirect(l_put[:]), a_sb[t][:], COPY)
 
         pg = sb.tile([P, PACK, O], F32, name="pg", align_bytes=64)

from contextlib import ExitStack

import concourse.mybir as mybir

K, T, J, R, C, O, N = 512, 1024, 256, 512, 512, 128, 256
FLOPS = 2 * K * J * R * 2 + 2 * N * O * (R + K)

F32 = mybir.dt.float32
BF16 = mybir.dt.bfloat16
I32 = mybir.dt.int32
U32 = mybir.dt.uint32
U16 = mybir.dt.uint16
U8 = mybir.dt.uint8
E4M3 = mybir.dt.float8_e4m3fn_x4
E5M2 = mybir.dt.float8_e5m2_x4
E2M1 = mybir.dt.float4_e2m1fn_x4
COPY = mybir.ActivationFunctionType.Copy
MAX = mybir.AluOpType.max

P = 128
PACK = 4
QUADS = 4


def load_scale_rows(queue, plane, scales):
    for q in range(QUADS):
        queue.dma_start(
            out=plane[32 * q : 32 * q + 4, :].bitcast(I32),
            in_=scales[0, 4 * q : 4 * q + 4, :].bitcast(I32),
        )


def deal_columns(copy, dealt, given, run, slices):
    copy(
        out=dealt.rearrange("p (t c i) -> p c t i", t=PACK, i=run)[:, :, slices, :],
        in_=given.rearrange("p (c i t) -> p c t i", t=PACK, i=run)[:, :, slices, :],
    )


def tile_list_boardweighed_twow_further_plain_kernel(
    tc, xt_words, xt_scales, w_words, w_scales, w2_words, w2_scales, sa, wb_words, wb_scales,
    ws_words, ws_scales, offs, offs2, offs3, offs4, offs5, out,
):
    nc = tc.nc
    with ExitStack() as ctx:
        lists = ctx.enter_context(tc.tile_pool(name="lists", bufs=1))
        sb = ctx.enter_context(tc.tile_pool(name="sb", bufs=1))
        ps = ctx.enter_context(tc.psum_pool(name="ps", bufs=1))

        l_tok = lists.tile([P, J // 16], U16, name="l_tok")
        l_put = lists.tile([P, J // 16], U16, name="l_put")
        l_board = lists.tile([P, O // 16], U16, name="l_board")
        l_slot = lists.tile([P, O // 16], U16, name="l_slot")
        l_short = lists.tile([P, O // 16], U16, name="l_short")

        xw = sb.tile([P, T], I32, name="xw", tag="a3", align_bytes=64)
        xs = sb.tile([P, T], U8, name="xs", tag="a1", align_bytes=64)
        ww = sb.tile([P, 2 * R], U8, name="ww", tag="ww", align_bytes=64)
        wsc = sb.tile([P, R], U8, name="wsc", align_bytes=64)
        wst = sb.tile([4, QUADS, R], U8, name="wst", align_bytes=64)
        w2w = sb.tile([P, R], I32, name="w2w", align_bytes=64)
        w2s = sb.tile([P, R], U8, name="w2s", align_bytes=64)
        wbw = sb.tile([P, 2 * N], U8, name="wbw", align_bytes=64)
        wbs = sb.tile([P, N], U8, name="wbs", align_bytes=64)
        wsw = sb.tile([P, 2 * N], U8, name="wsw", align_bytes=64)
        wss = sb.tile([P, N], U8, name="wss", align_bytes=64)
        sa_sb = sb.tile([P, PACK], F32, name="sa_sb", align_bytes=64)
        boards = [sb.tile([P, C], F32, name="board%d" % t, align_bytes=64) for t in range(PACK)]

        nc.gpsimd.memset(xs[:].bitcast(I32), 0)
        nc.gpsimd.memset(wsc[:].bitcast(I32), 0)
        nc.gpsimd.memset(w2s[:].bitcast(I32), 0)
        nc.gpsimd.memset(wbs[:].bitcast(I32), 0)
        nc.gpsimd.memset(wss[:].bitcast(I32), 0)
        for t in range(PACK):
            nc.vector.memset(boards[t][:], 0.0)

        nc.sync.dma_start(
            out=wst[:].bitcast(I32),
            in_=w_scales[0].bitcast(I32).rearrange("(q r) c -> r q c", r=4),
        )
        nc.sync.dma_start(l_tok[:], offs)
        load_scale_rows(nc.scalar, xs, xt_scales)
        nc.sync.dma_start(out=xw[:], in_=xt_words[0].rearrange("p n t -> p (n t)").bitcast(I32))
        nc.sync.dma_start(out=ww[:].bitcast(I32), in_=w_words[0].bitcast(I32))
        nc.sync.dma_start(l_short[:], offs5)
        nc.sync.dma_start(l_put[:], offs2)
        load_scale_rows(nc.sync, w2s, w2_scales)
        nc.sync.dma_start(out=w2w[:], in_=w2_words[0].rearrange("p n t -> p (n t)").bitcast(I32))
        nc.sync.dma_start(l_board[:], offs3)
        nc.sync.dma_start(out=sa_sb[:], in_=sa.rearrange("(p t) o -> p (t o)", t=PACK))
        nc.sync.dma_start(l_slot[:], offs4)
        nc.sync.dma_start(out=wsw[:].bitcast(I32), in_=ws_words[0].bitcast(I32))
        load_scale_rows(nc.sync, wss, ws_scales)
        nc.sync.dma_start(out=wbw[:].bitcast(I32), in_=wb_words[0].bitcast(I32))
        load_scale_rows(nc.sync, wbs, wb_scales)

        for q in range(QUADS):
            nc.vector.tensor_copy(
                out=wsc[32 * q : 32 * q + 4, :].bitcast(I32), in_=wst[:, q, :].bitcast(I32)
            )
        wwp = sb.tile([P, 2 * R], U8, name="wwp", align_bytes=64)
        wsp = sb.tile([P, R], U8, name="wsp", align_bytes=64)
        deal_columns(nc.scalar.copy, wwp[:].bitcast(U16), ww[:].bitcast(U16), 8, slice(0, 2))
        deal_columns(nc.scalar.copy, wwp[:].bitcast(U16), ww[:].bitcast(U16), 8, slice(2, 4))
        deal_columns(nc.vector.tensor_copy, wsp[:], wsc[:], 16, slice(0, 4))

        xgs = sb.tile([P, J], U8, name="xgs", align_bytes=64)
        xgw = sb.tile([P, J], U32, name="xgw", align_bytes=64)
        nc.vector.tensor_copy(xgs[:], xs[:].indirect(l_tok[:]))
        nc.vector.tensor_copy(xgw[:], xw[:].bitcast(U32).indirect(l_tok[:]))

        a_ps = [ps.tile([P, J], F32, name="a_ps%d" % t) for t in range(PACK)]
        for t in range(PACK):
            nc.tensor.matmul_mx(
                out=a_ps[t][:],
                lhsT=wwp[:, 2 * P * t : 2 * P * (t + 1)].bitcast(E2M1),
                lhsT_scale=wsp[:, P * t : P * (t + 1)],
                rhs=xgw[:].bitcast(E5M2),
                rhs_scale=xgs[:],
                start=True,
                stop=True,
            )

        x5s = sb.tile([P, O], U8, name="x5s", tag="ww", align_bytes=64)
        x5w = sb.tile([P, O], U32, name="x5w", align_bytes=64)
        nc.vector.tensor_copy(x5s[:], xs[:].indirect(l_short[:]))
        nc.vector.tensor_copy(x5w[:], xw[:].bitcast(U32).indirect(l_short[:]))

        w2wp = sb.tile([P, R], I32, name="w2wp", align_bytes=64)
        w2sp = sb.tile([P, R], U8, name="w2sp", align_bytes=64)
        deal_columns(nc.gpsimd.tensor_copy, w2sp[:], w2s[:], 16, slice(0, 4))
        deal_columns(nc.gpsimd.tensor_copy, w2wp[:], w2w[:], 4, slice(0, 4))
        b_ps = [ps.tile([P, 2, J], F32, name="b_ps%d" % h, tag="bank%d" % h) for h in range(2)]
        for t in range(PACK):
            nc.tensor.matmul_mx(
                out=b_ps[t // 2][:, t % 2, :],
                lhsT=w2wp[:, P * t : P * (t + 1)].bitcast(E4M3),
                lhsT_scale=w2sp[:, P * t : P * (t + 1)],
                rhs=xgw[:].bitcast(E5M2),
                rhs_scale=xgs[:],
                start=True,
                stop=True,
            )

        a_sb = [sb.tile([P, J], F32, name="a_sb%d" % t, tag="a%d" % t, align_bytes=64) for t in range(PACK)]
        for t in range(PACK):
            if t % 2 == 1:
                nc.vector.tensor_copy(a_sb[t][:], a_ps[t][:])
            else:
                nc.scalar.activation(a_sb[t][:], a_ps[t][:], COPY)
        for t in range(PACK):
            if t % 2 == 1:
                nc.vector.tensor_copy(boards[t][:].indirect(l_put[:]), a_sb[t][:])
            else:
                nc.scalar.activation(boards[t][:].indirect(l_put[:]), a_sb[t][:], COPY)

        pg = sb.tile([P, PACK, O], F32, name="pg", align_bytes=64)
        b_sb = [sb.tile([P, 2, J], F32, name="b_sb%d" % h, align_bytes=64) for h in range(2)]
        bg = sb.tile([P, PACK, O], F32, name="bg", align_bytes=64)
        for t in (0, 2, 1, 3):
            nc.scalar.activation(
                pg[:, t, :], boards[t][:].indirect(l_board[:]), COPY, scale=sa_sb[:, t : t + 1]
            )
        for h in range(2):
            nc.vector.tensor_copy(b_sb[h][:], b_ps[h][:])
        nc.scalar.activation(bg[:, 0, :], b_sb[0][:, 0, :].indirect(l_slot[:]), COPY)
        for t in range(1, PACK):
            nc.vector.tensor_copy(bg[:, t, :], b_sb[t // 2][:, t % 2, :].indirect(l_slot[:]))

        y_ps = [ps.tile([P, O], F32, name="y_ps%d" % h, tag="bank%d" % h) for h in range(2)]
        for h in range(2):
            nc.tensor.matmul_mx(
                out=y_ps[h][:],
                lhsT=wsw[:, 2 * P * h : 2 * P * (h + 1)].bitcast(E2M1),
                lhsT_scale=wss[:, P * h : P * (h + 1)],
                rhs=x5w[:].bitcast(E5M2),
                rhs_scale=x5s[:],
                start=True,
                stop=False,
            )

        hid = sb.tile([P, O, PACK], BF16, name="hid", align_bytes=64)
        nc.vector.tensor_tensor(
            hid[:].rearrange("p (c i) t -> p c t i", i=4),
            pg[:].rearrange("p t (c i) -> p c t i", i=4),
            bg[:].rearrange("p t (c i) -> p c t i", i=4),
            MAX,
        )
        hq = sb.tile([P, O], U32, name="hq", align_bytes=64)
        hs = sb.tile([P, O], U8, name="hs", align_bytes=64)
        nc.vector.quantize_mx(out=hq[:].bitcast(E4M3), scales=hs[:], in_=hid[:].rearrange("p o t -> p (o t)"))

        y_sb = [sb.tile([P, O], F32, name="y_sb%d" % h, align_bytes=64) for h in range(2)]
        for h in range(2):
            nc.tensor.matmul_mx(
                out=y_ps[h][:],
                lhsT=wbw[:, 2 * P * h : 2 * P * (h + 1)].bitcast(E2M1),
                lhsT_scale=wbs[:, P * h : P * (h + 1)],
                rhs=hq[:].bitcast(E4M3),
                rhs_scale=hs[:],
                start=False,
                stop=True,
            )
        nc.vector.tensor_copy(y_sb[0][:], y_ps[0][:])
        nc.sync.dma_start(out=out[0:P, :], in_=y_sb[0][:])
        nc.scalar.activation(y_sb[1][:], y_ps[1][:], COPY)
        nc.scalar.dma_start(out=out[P : 2 * P, :], in_=y_sb[1][:])
